import numpy as np
import ml_dtypes


def mxq(x, axis, fmt="e4m3"):
    dtype, down = {"e4m3": (ml_dtypes.float8_e4m3fn, 7), "e5m2": (ml_dtypes.float8_e5m2, 14)}[fmt]
    v = np.moveaxis(np.asarray(x, np.float32).astype(ml_dtypes.bfloat16).astype(np.float64), axis, -1)
    blocks = v.reshape(v.shape[:-1] + (-1, 32))
    amax = np.abs(blocks).max(-1, keepdims=True)
    byte = np.maximum(np.where(amax > 0, np.frexp(amax)[1] - 1 + 127, 0) - down, 1)
    scale = np.exp2(byte - 127.0)
    codes = (blocks / scale).astype(np.float32).astype(dtype).astype(np.float64)
    return np.moveaxis((codes * scale).reshape(v.shape), -1, axis)


WIDE = False


def mx_kscale(k):
    if not WIDE:
        return np.ones(k)
    levels = np.array([10, -10, 5, -5, 0])
    if k % 512:
        return np.exp2(np.random.permutation(np.resize(levels, k // 32))).repeat(32)
    a = np.empty((k // 512, 16))
    for p in range(k // 512):
        a[p, :8] = np.random.permutation(np.resize(levels, 8))
        for g in range(8):
            far = levels[np.abs(levels - a[p, g]) >= 10]
            a[p, g + 8] = far[np.random.randint(len(far))]
    return np.exp2(a.ravel()).repeat(32)


def f64(x):
    return np.asarray(x).astype(np.float64)


def striped(idx):
    return np.tile(idx.reshape(-1, 16).T, (8, 1)).astype(np.uint16)


def unstriped(offs):
    return offs[:16].T.reshape(-1).astype(np.int64)


def striped8(idx):
    return np.concatenate([x.reshape(-1, 16).T for x in idx]).astype(np.uint16)


def runs(offs, k):
    lists = np.stack([offs[16 * r : 16 * r + 16].T.reshape(-1) for r in range(8)]).astype(np.int64)
    return lists[np.arange(k) % 512 // 64]


def pack_weight(w):
    k, n = w.shape
    w = f64(np.asarray(w, np.float32).astype(ml_dtypes.bfloat16)).reshape(k // 32, 32, n)
    amax = np.abs(w).max(1)
    byte = np.clip(np.where(amax > 0, np.frexp(amax)[1] - 1 + 127 - 7, 1), 1, 254)
    scaled = (w * np.exp2(127.0 - byte)[:, None, :]).reshape(k, n).astype(np.float32)
    words = np.ascontiguousarray(scaled.reshape(k // 512, 128, 4, n).transpose(0, 1, 3, 2)).astype(ml_dtypes.float8_e4m3fn).view(np.uint8)
    return words, np.ascontiguousarray(byte.astype(np.uint8).reshape(k // 512, 16, n))


def unpack_weight(words, scales):
    g, p, n, _ = words.shape
    vals = np.ascontiguousarray(words).view(ml_dtypes.float8_e4m3fn).astype(np.float64) * np.repeat(np.exp2(scales.astype(np.float64) - 127.0), 8, axis=1)[..., None]
    return vals.transpose(0, 1, 3, 2).reshape(g * 512, n)


def sigmoid(v):
    return 1.0 / (1.0 + np.exp(-np.maximum(v, -700.0)))


K, T, S, N, G, H = 512, 2048, 256, 512, 2048, 512


def setup_inputs():
    n = np.random.standard_normal
    s = mx_kscale(K)[:, None]
    u = mx_kscale(K)
    packed_xT = pack_weight(n((K, T)) * s)
    packed_dT = pack_weight(n((K, G)) / s)
    return {
        "x_words": packed_xT[0],
        "x_scales": packed_xT[1],
        "d_words": packed_dT[0],
        "d_scales": packed_dT[1],
        "gn": (np.random.uniform(0.5, 1.5, (H, 1)) * u[:, None]).astype(np.float32),
        "w1": (n((H, N)) / np.sqrt(H) / u[:, None]).astype(np.float32),
        "sl": np.random.uniform(1.0, 2.0, (N, 1)).astype(np.float32),
        "th": (0.5 * n((N, 1))).astype(np.float32),
        "offs": striped8(np.random.randint(0, T, (8, S))),
        "ci": striped(np.random.permutation(G)[:H]),
        "n1": striped(np.random.permutation(S)),
        "n2": striped(np.random.permutation(S)),
        "n3": striped(np.random.permutation(S)),
        "n4": striped(np.random.permutation(S)),
    }


def reference(x_words, x_scales, d_words, d_scales, gn, w1, sl, th, offs, ci, n1, n2, n3, n4):
    d_ci = unpack_weight(d_words, d_scales)[:, unstriped(ci)]
    xq = unpack_weight(x_words, x_scales)[np.arange(K)[:, None], runs(offs, K)]
    s = 0.0625 * (d_ci.T @ xq)
    st = np.maximum(s, s[:, unstriped(n1)])
    ds = np.zeros((H, S))
    ds[:, unstriped(n2)] = st
    z = f64(gn) * (ds - s)
    h = mxq(f64(w1), 0, "e4m3").T @ mxq(z, 0, "e4m3")
    ds2 = np.zeros((N, S))
    ds2[:, unstriped(n3)] = h
    sg = sigmoid(f64(sl) * (ds2[:, unstriped(n4)] - f64(th)))
    return h * sg

@@ -1,0 +1,197 @@
+from contextlib import ExitStack
+
+import concourse.mybir as mybir
+
+F32 = mybir.dt.float32
+BF16 = mybir.dt.bfloat16
+I32 = mybir.dt.int32
+U32 = mybir.dt.uint32
+U16 = mybir.dt.uint16
+U8 = mybir.dt.uint8
+FP8X4 = mybir.dt.float8_e4m3fn_x4
+ALU = mybir.AluOpType
+ACT = mybir.ActivationFunctionType
+
+P = 128
+T = 2048
+S = 256
+H = 512
+N = 512
+PACK = 4
+WIN = 2 * S
+HALF = S // 2
+FLOPS = 2 * 512 * H * S + 2 * H * N * S
+
+
+def tile_picked_hwlsendhoperl_none_p_kernel(
+    tc, x_words, x_scales, d_words, d_scales, gn, w1, sl, th, offs, ci, n1, n2, n3, n4, out
+):
+    nc = tc.nc
+    with ExitStack() as ctx:
+        keep = ctx.enter_context(tc.tile_pool(name="keep", bufs=1))
+        psum = ctx.enter_context(tc.psum_pool(name="psum", bufs=1))
+
+        offs_t = keep.tile([P, S // 16], U16, name="offs_t")
+        ci_t = keep.tile([P, H // 16], U16, name="ci_t")
+        n1_t = keep.tile([P, S // 16], U16, name="n1_t")
+        n2_t = keep.tile([P, S // 16], U16, name="n2_t")
+        n3_t = keep.tile([P, S // 16], U16, name="n3_t")
+        n4_t = keep.tile([P, S // 16], U16, name="n4_t")
+
+        xs_win = keep.tile([P, T], U8, name="xs_win")
+        ds_win = keep.tile([P, T], U8, name="ds_win")
+        xw_win = keep.tile([P, T], I32, name="xw_win")
+        dw_win = keep.tile([P, T], I32, name="dw_win")
+        nc.vector.memset(xs_win[:].bitcast(I32), 0)
+        nc.vector.memset(ds_win[:].bitcast(I32), 0)
+        xs_rows = x_scales[0].bitcast(I32)
+        ds_rows = d_scales[0].bitcast(I32)
+        nc.sync.dma_start(out=offs_t[:], in_=offs)
+        for c in range(2):
+            nc.scalar.dma_start(out=xs_win[:].bitcast(I32)[c:P:16, :], in_=xs_rows[c:16:2, :])
+        for i in range(4):
+            nc.gpsimd.dma_start(out=ds_win[:].bitcast(I32)[i:P:32, :], in_=ds_rows[i:16:4, :])
+        nc.sync.dma_start(out=dw_win[:], in_=d_words[0].rearrange("p c r -> p (c r)").bitcast(I32))
+        nc.sync.dma_start(out=ci_t[:], in_=ci)
+        nc.sync.dma_start(out=n1_t[:], in_=n1)
+        nc.sync.dma_start(out=xw_win[:], in_=x_words[0].rearrange("p c r -> p (c r)").bitcast(I32))
+        nc.sync.dma_start(out=n2_t[:], in_=n2)
+        nc.sync.dma_start(out=n3_t[:], in_=n3)
+        nc.sync.dma_start(out=n4_t[:], in_=n4)
+        w_raw = keep.tile([P, PACK, N], F32, name="w_raw")
+        nc.sync.dma_start(out=w_raw[:], in_=w1.rearrange("(p j) n -> p j n", j=PACK))
+        gn_t = keep.tile([P, PACK], F32, name="gn_t")
+        nc.sync.dma_start(out=gn_t[:], in_=gn.rearrange("(p j) o -> p (j o)", j=PACK))
+        sl_t = keep.tile([P, PACK, 1], F32, name="sl_t")
+        th_t = keep.tile([P, PACK, 1], F32, name="th_t")
+        with nc.allow_non_contiguous_dma(reason="one value a row"):
+            nc.sync.dma_start(out=sl_t[:], in_=sl.rearrange("(u p) o -> p u o", p=P))
+            nc.sync.dma_start(out=th_t[:], in_=th.rearrange("(u p) o -> p u o", p=P))
+
+        xs_g = keep.tile([P, S], U8, name="xs_g")
+        nc.vector.tensor_copy(out=xs_g[:], in_=xs_win[:].indirect(offs_t[:]))
+        xs_p = keep.tile([P, S], U8, name="xs_p", align_bytes=64)
+        nc.vector.tensor_copy(out=xs_p[:].bitcast(I32), in_=xs_g[:].bitcast(I32))
+        for c in range(2):
+            nc.scalar.dma_start(
+                out=xs_p[:].bitcast(I32)[2 + c : P : 32, :], in_=xs_g[:].bitcast(I32)[16 + c : P : 32, :]
+            )
+        ds_g = keep.tile([P, H], U8, name="ds_g", align_bytes=64)
+        nc.vector.tensor_copy(
+            out=ds_g[:].rearrange("p (t m) -> p m t", t=PACK), in_=ds_win[:].indirect(ci_t[:])
+        )
+        dw_g = keep.tile([P, H], U32, name="dw_g", align_bytes=64)
+        nc.vector.tensor_copy(
+            out=dw_g[:].rearrange("p (t m) -> p m t", t=PACK), in_=dw_win[:].bitcast(U32).indirect(ci_t[:])
+        )
+        xw_g = keep.tile([P, S], U32, name="xw_g", align_bytes=64)
+        nc.vector.tensor_copy(out=xw_g[:], in_=xw_win[:].bitcast(U32).indirect(offs_t[:]))
+
+        s_win = []
+        for t in range(PACK):
+            cols = slice(t * P, (t + 1) * P)
+            s_ps = psum.tile([P, S], F32, name=f"s_ps{t}", tag=f"bank{t}")
+            nc.tensor.matmul_mx(
+                out=s_ps[:],
+                lhsT=dw_g[:, cols].bitcast(FP8X4),
+                lhsT_scale=ds_g[:, cols],
+                rhs=xw_g[:].bitcast(FP8X4),
+                rhs_scale=xs_p[:],
+                start=True,
+                stop=True,
+            )
+            win = keep.tile([P, WIN], F32, name=f"s_win{t}")
+            nc.vector.tensor_scalar(
+                out=win[:, :S], in0=s_ps[:], scalar1=0.0625, scalar2=None, op0=ALU.mult
+            )
+            s_win.append(win)
+        fetched = []
+        for t in range(PACK):
+            f = keep.tile([P, S], F32, name=f"fetched{t}")
+            nc.scalar.activation(out=f[:], in_=s_win[t][:].indirect(n1_t[:]), func=ACT.Copy)
+            fetched.append(f)
+        st = []
+        for t in range(PACK):
+            m = keep.tile([P, S], F32, name=f"st{t}")
+            nc.vector.tensor_tensor(out=m[:], in0=s_win[t][:, :S], in1=fetched[t][:], op=ALU.max)
+            st.append(m)
+        sent = []
+        for t in range(PACK):
+            win = keep.tile([P, WIN], F32, name=f"sent{t}")
+            nc.scalar.activation(out=win[:].indirect(n2_t[:]), in_=st[t][:], func=ACT.Copy)
+            sent.append(win)
+
+        w_codes = keep.tile([P, N], U32, name="w_codes", align_bytes=64)
+        w_scales = keep.tile([P, N], U8, name="w_scales", align_bytes=64)
+        for u in range(PACK):
+            cols = slice(u * P, (u + 1) * P)
+            w_bf = keep.tile([P, P, PACK], BF16, name=f"w_bf{u}", tag=f"stage{u}", align_bytes=64)
+            nc.vector.tensor_copy(
+                out=w_bf[:].rearrange("p (c i) j -> p c j i", i=4),
+                in_=w_raw[:, :, cols].rearrange("p j (c i) -> p c j i", i=4),
+            )
+            nc.vector.quantize_mx(
+                out=w_codes[:, cols].bitcast(FP8X4),
+                scales=w_scales[:, cols],
+                in_=w_bf[:].rearrange("p c j -> p (c j)"),
+            )
+        bias_t = keep.tile([P, PACK, 1], F32, name="bias_t")
+        nc.vector.scalar_tensor_tensor(
+            out=bias_t[:], in0=sl_t[:], scalar=-1.0, in1=th_t[:], op0=ALU.mult, op1=ALU.mult
+        )
+
+        halves = [slice(0, HALF), slice(HALF, S)]
+        z_bf = [keep.tile([P, HALF, PACK], BF16, name=f"z_bf{a}", align_bytes=64) for a in range(2)]
+        for t in range(PACK):
+            diff = keep.tile([P, S], F32, name=f"diff{t}", tag=f"stage{t}", align_bytes=64)
+            for a in range(2):
+                nc.vector.tensor_tensor(
+                    out=diff[:, halves[a]], in0=sent[t][:, halves[a]], in1=s_win[t][:, halves[a]], op=ALU.subtract
+                )
+            for a in range(2):
+                nc.vector.tensor_scalar(
+                    out=z_bf[a][:, :, t], in0=diff[:, halves[a]], scalar1=gn_t[:, t : t + 1], scalar2=None, op0=ALU.mult
+                )
+        h_sb = [keep.tile([P, S], F32, name=f"h_sb{u}") for u in range(PACK)]
+        for a in range(2):
+            z_codes = keep.tile([P, HALF], U32, name=f"z_codes{a}", align_bytes=64)
+            z_scales = keep.tile([P, HALF], U8, name=f"z_scales{a}", align_bytes=64)
+            nc.vector.quantize_mx(
+                out=z_codes[:].bitcast(FP8X4),
+                scales=z_scales[:],
+                in_=z_bf[a][:].rearrange("p c j -> p (c j)"),
+            )
+            for u in range(PACK):
+                cols = slice(u * P, (u + 1) * P)
+                h_ps = psum.tile([P, HALF], F32, name=f"h_ps{a}{u}", tag=f"bank{(1 - a) * PACK + u}")
+                nc.tensor.matmul_mx(
+                    out=h_ps[:],
+                    lhsT=w_codes[:, cols].bitcast(FP8X4),
+                    lhsT_scale=w_scales[:, cols],
+                    rhs=z_codes[:].bitcast(FP8X4),
+                    rhs_scale=z_scales[:],
+                    start=True,
+                    stop=True,
+                )
+                nc.vector.tensor_copy(out=h_sb[u][:, halves[a]], in_=h_ps[:])
+
+        for u in range(PACK):
+            win = keep.tile([P, WIN], F32, name=f"sent2_{u}")
+            if u == 0:
+                for a in range(2):
+                    nc.scalar.activation(
+                        out=win[:].indirect(n3_t[:, a * 8 : (a + 1) * 8]), in_=h_sb[u][:, halves[a]], func=ACT.Copy
+                    )
+            else:
+                nc.scalar.activation(out=win[:].indirect(n3_t[:]), in_=h_sb[u][:], func=ACT.Copy)
+            sg = keep.tile([P, S], F32, name=f"sg{u}")
+            nc.scalar.activation(
+                out=sg[:],
+                in_=win[:].indirect(n4_t[:]),
+                func=ACT.Sigmoid,
+                scale=sl_t[:, u, :],
+                bias=bias_t[:, u, :],
+            )
+            res = keep.tile([P, S], F32, name=f"res{u}")
+            nc.vector.tensor_tensor(out=res[:], in0=h_sb[u][:], in1=sg[:], op=ALU.mult)
+            nc.sync.dma_start(out=out[u * P : (u + 1) * P, :], in_=res[:])

@@ -38,35 +38,27 @@ def tile_picked_hwlsendhoperl_none_p_kernel(
         n3_t = keep.tile([P, S // 16], U16, name="n3_t")
         n4_t = keep.tile([P, S // 16], U16, name="n4_t")
 
-        xs_win = keep.tile([P, T], U8, name="xs_win")
-        ds_win = keep.tile([P, T], U8, name="ds_win")
-        xw_win = keep.tile([P, T], I32, name="xw_win")
-        dw_win = keep.tile([P, T], I32, name="dw_win")
+        xs_win = keep.tile([P, T], U8, name="xs_win", tag="slot_a", align_bytes=64)
+        ds_win = keep.tile([P, T], U8, name="ds_win", tag="slot_b", align_bytes=64)
+        xw_win = keep.tile([P, T], I32, name="xw_win", tag="slot_d")
+        dw_win = keep.tile([P, T], I32, name="dw_win", tag="slot_c")
         nc.vector.memset(xs_win[:].bitcast(I32), 0)
         nc.vector.memset(ds_win[:].bitcast(I32), 0)
         xs_rows = x_scales[0].bitcast(I32)
         ds_rows = d_scales[0].bitcast(I32)
         nc.sync.dma_start(out=offs_t[:], in_=offs)
-        for c in range(2):
-            nc.scalar.dma_start(out=xs_win[:].bitcast(I32)[c:P:16, :], in_=xs_rows[c:16:2, :])
-        for i in range(4):
-            nc.gpsimd.dma_start(out=ds_win[:].bitcast(I32)[i:P:32, :], in_=ds_rows[i:16:4, :])
-        nc.sync.dma_start(out=dw_win[:], in_=d_words[0].rearrange("p c r -> p (c r)").bitcast(I32))
         nc.sync.dma_start(out=ci_t[:], in_=ci)
+        nc.sync.dma_start(out=dw_win[:], in_=d_words[0].rearrange("p c r -> p (c r)").bitcast(I32))
         nc.sync.dma_start(out=n1_t[:], in_=n1)
         nc.sync.dma_start(out=xw_win[:], in_=x_words[0].rearrange("p c r -> p (c r)").bitcast(I32))
         nc.sync.dma_start(out=n2_t[:], in_=n2)
         nc.sync.dma_start(out=n3_t[:], in_=n3)
         nc.sync.dma_start(out=n4_t[:], in_=n4)
-        w_raw = keep.tile([P, PACK, N], F32, name="w_raw")
-        nc.sync.dma_start(out=w_raw[:], in_=w1.rearrange("(p j) n -> p j n", j=PACK))
-        gn_t = keep.tile([P, PACK], F32, name="gn_t")
-        nc.sync.dma_start(out=gn_t[:], in_=gn.rearrange("(p j) o -> p (j o)", j=PACK))
-        sl_t = keep.tile([P, PACK, 1], F32, name="sl_t")
-        th_t = keep.tile([P, PACK, 1], F32, name="th_t")
-        with nc.allow_non_contiguous_dma(reason="one value a row"):
-            nc.sync.dma_start(out=sl_t[:], in_=sl.rearrange("(u p) o -> p u o", p=P))
-            nc.sync.dma_start(out=th_t[:], in_=th.rearrange("(u p) o -> p u o", p=P))
+        for c in range(2):
+            nc.scalar.dma_start(out=xs_win[:].bitcast(I32)[c:P:16, :], in_=xs_rows[c:16:2, :])
+        for i in range(4):
+            queue = nc.scalar if i < 3 else nc.gpsimd
+            queue.dma_start(out=ds_win[:].bitcast(I32)[i:P:32, :], in_=ds_rows[i:16:4, :])
 
         xs_g = keep.tile([P, S], U8, name="xs_g")
         nc.vector.tensor_copy(out=xs_g[:], in_=xs_win[:].indirect(offs_t[:]))
@@ -76,16 +68,27 @@ def tile_picked_hwlsendhoperl_none_p_kernel(
             nc.scalar.dma_start(
                 out=xs_p[:].bitcast(I32)[2 + c : P : 32, :], in_=xs_g[:].bitcast(I32)[16 + c : P : 32, :]
             )
+        dw_g = keep.tile([P, H], U32, name="dw_g", tag="slot_a", align_bytes=64)
+        nc.vector.tensor_copy(
+            out=dw_g[:].rearrange("p (t m) -> p m t", t=PACK), in_=dw_win[:].bitcast(U32).indirect(ci_t[:])
+        )
         ds_g = keep.tile([P, H], U8, name="ds_g", align_bytes=64)
         nc.vector.tensor_copy(
             out=ds_g[:].rearrange("p (t m) -> p m t", t=PACK), in_=ds_win[:].indirect(ci_t[:])
         )
-        dw_g = keep.tile([P, H], U32, name="dw_g", align_bytes=64)
-        nc.vector.tensor_copy(
-            out=dw_g[:].rearrange("p (t m) -> p m t", t=PACK), in_=dw_win[:].bitcast(U32).indirect(ci_t[:])
-        )
-        xw_g = keep.tile([P, S], U32, name="xw_g", align_bytes=64)
+        xw_g = keep.tile([P, S], U32, name="xw_g", tag="slot_b", align_bytes=64)
         nc.vector.tensor_copy(out=xw_g[:], in_=xw_win[:].bitcast(U32).indirect(offs_t[:]))
+
+        w_raw = keep.tile([P, PACK, N], F32, name="w_raw", tag="slot_c")
+        nc.sync.dma_start(out=w_raw[:], in_=w1.rearrange("(p j) n -> p j n", j=PACK))
+        rowvals = keep.tile([P, 3, 8, 1], F32, name="rowvals", tag="slot_d")
+        gn_t = rowvals[:, 0, :PACK, :]
+        sl_t = rowvals[:, 1, :PACK, :]
+        th_t = rowvals[:, 2, :PACK, :]
+        with nc.allow_non_contiguous_dma(reason="one value a row"):
+            nc.sync.dma_start(out=gn_t, in_=gn.rearrange("(p j) o -> p j o", j=PACK))
+            nc.sync.dma_start(out=sl_t, in_=sl.rearrange("(u p) o -> p u o", p=P))
+            nc.sync.dma_start(out=th_t, in_=th.rearrange("(u p) o -> p u o", p=P))
 
         s_win = []
         for t in range(PACK):
@@ -105,15 +108,13 @@ def tile_picked_hwlsendhoperl_none_p_kernel(
                 out=win[:, :S], in0=s_ps[:], scalar1=0.0625, scalar2=None, op0=ALU.mult
             )
             s_win.append(win)
-        fetched = []
+        fetched = keep.tile([P, PACK, S], F32, name="fetched", tag="stage", align_bytes=64)
         for t in range(PACK):
-            f = keep.tile([P, S], F32, name=f"fetched{t}")
-            nc.scalar.activation(out=f[:], in_=s_win[t][:].indirect(n1_t[:]), func=ACT.Copy)
-            fetched.append(f)
+            nc.scalar.activation(out=fetched[:, t, :], in_=s_win[t][:].indirect(n1_t[:]), func=ACT.Copy)
         st = []
         for t in range(PACK):
             m = keep.tile([P, S], F32, name=f"st{t}")
-            nc.vector.tensor_tensor(out=m[:], in0=s_win[t][:, :S], in1=fetched[t][:], op=ALU.max)
+            nc.vector.tensor_tensor(out=m[:], in0=s_win[t][:, :S], in1=fetched[:, t, :], op=ALU.max)
             st.append(m)
         sent = []
         for t in range(PACK):
@@ -123,34 +124,32 @@ def tile_picked_hwlsendhoperl_none_p_kernel(
 
         w_codes = keep.tile([P, N], U32, name="w_codes", align_bytes=64)
         w_scales = keep.tile([P, N], U8, name="w_scales", align_bytes=64)
+        w_bf = keep.tile([P, N, PACK], BF16, name="w_bf", tag="stage", align_bytes=64)
         for u in range(PACK):
             cols = slice(u * P, (u + 1) * P)
-            w_bf = keep.tile([P, P, PACK], BF16, name=f"w_bf{u}", tag=f"stage{u}", align_bytes=64)
             nc.vector.tensor_copy(
-                out=w_bf[:].rearrange("p (c i) j -> p c j i", i=4),
+                out=w_bf[:, cols, :].rearrange("p (c i) j -> p c j i", i=4),
                 in_=w_raw[:, :, cols].rearrange("p j (c i) -> p c j i", i=4),
             )
-            nc.vector.quantize_mx(
-                out=w_codes[:, cols].bitcast(FP8X4),
-                scales=w_scales[:, cols],
-                in_=w_bf[:].rearrange("p c j -> p (c j)"),
-            )
-        bias_t = keep.tile([P, PACK, 1], F32, name="bias_t")
-        nc.vector.scalar_tensor_tensor(
-            out=bias_t[:], in0=sl_t[:], scalar=-1.0, in1=th_t[:], op0=ALU.mult, op1=ALU.mult
+        nc.vector.quantize_mx(
+            out=w_codes[:].bitcast(FP8X4), scales=w_scales[:], in_=w_bf[:].rearrange("p c j -> p (c j)")
         )
+        bias_t = keep.tile([P, PACK, 1], F32, name="bias_t")
+        slth = keep.tile([P, PACK, 1], F32, name="slth")
+        nc.gpsimd.tensor_tensor(out=slth[:], in0=sl_t, in1=th_t, op=ALU.mult)
+        nc.gpsimd.tensor_scalar(out=bias_t[:], in0=slth[:], scalar1=-1.0, scalar2=0.0, op0=ALU.mult, op1=ALU.add)
 
         halves = [slice(0, HALF), slice(HALF, S)]
         z_bf = [keep.tile([P, HALF, PACK], BF16, name=f"z_bf{a}", align_bytes=64) for a in range(2)]
+        diff = keep.tile([P, PACK, S], F32, name="diff", tag="stage", align_bytes=64)
         for t in range(PACK):
-            diff = keep.tile([P, S], F32, name=f"diff{t}", tag=f"stage{t}", align_bytes=64)
             for a in range(2):
                 nc.vector.tensor_tensor(
-                    out=diff[:, halves[a]], in0=sent[t][:, halves[a]], in1=s_win[t][:, halves[a]], op=ALU.subtract
+                    out=diff[:, t, halves[a]], in0=sent[t][:, halves[a]], in1=s_win[t][:, halves[a]], op=ALU.subtract
                 )
             for a in range(2):
                 nc.vector.tensor_scalar(
-                    out=z_bf[a][:, :, t], in0=diff[:, halves[a]], scalar1=gn_t[:, t : t + 1], scalar2=None, op0=ALU.mult
+                    out=z_bf[a][:, :, t], in0=diff[:, t, halves[a]], scalar1=gn_t[:, t, :], scalar2=None, op0=ALU.mult
                 )
         h_sb = [keep.tile([P, S], F32, name=f"h_sb{u}") for u in range(PACK)]
         for a in range(2):

@@ -20,7 +20,14 @@ N = 512
 PACK = 4
 WIN = 2 * S
 HALF = S // 2
+EARLY = T // 4
 FLOPS = 2 * 512 * H * S + 2 * H * N * S
+
+
+def place_scale_rows(nc, placed, gathered):
+    nc.vector.tensor_copy(out=placed[:].bitcast(I32), in_=gathered[:].bitcast(I32))
+    for i in range(1, 4):
+        nc.sync.dma_start(out=placed[:].bitcast(I32)[i:P:32, :], in_=gathered[:].bitcast(I32)[8 * i : P : 32, :])
 
 
 def tile_picked_hwlsendhoperl_none_p_kernel(
@@ -44,37 +51,32 @@ def tile_picked_hwlsendhoperl_none_p_kernel(
         dw_win = keep.tile([P, T], I32, name="dw_win", tag="slot_c")
         nc.vector.memset(xs_win[:].bitcast(I32), 0)
         nc.vector.memset(ds_win[:].bitcast(I32), 0)
-        xs_rows = x_scales[0].bitcast(I32)
-        ds_rows = d_scales[0].bitcast(I32)
         nc.sync.dma_start(out=offs_t[:], in_=offs)
         nc.sync.dma_start(out=ci_t[:], in_=ci)
-        nc.sync.dma_start(out=dw_win[:], in_=d_words[0].rearrange("p c r -> p (c r)").bitcast(I32))
+        d_rows = d_words[0].rearrange("p c r -> p (c r)").bitcast(I32)
+        nc.sync.dma_start(out=dw_win[:, :EARLY], in_=d_rows[:, :EARLY])
+        nc.sync.dma_start(out=xs_win[:].bitcast(I32)[0:P:8, :], in_=x_scales[0].bitcast(I32))
+        nc.sync.dma_start(out=ds_win[:].bitcast(I32)[0:P:8, :], in_=d_scales[0].bitcast(I32))
+        nc.sync.dma_start(out=dw_win[:, EARLY:], in_=d_rows[:, EARLY:])
         nc.sync.dma_start(out=n1_t[:], in_=n1)
-        nc.sync.dma_start(out=xw_win[:], in_=x_words[0].rearrange("p c r -> p (c r)").bitcast(I32))
         nc.sync.dma_start(out=n2_t[:], in_=n2)
         nc.sync.dma_start(out=n3_t[:], in_=n3)
+        nc.sync.dma_start(out=xw_win[:], in_=x_words[0].rearrange("p c r -> p (c r)").bitcast(I32))
         nc.sync.dma_start(out=n4_t[:], in_=n4)
-        for c in range(2):
-            nc.scalar.dma_start(out=xs_win[:].bitcast(I32)[c:P:16, :], in_=xs_rows[c:16:2, :])
-        for i in range(4):
-            queue = nc.scalar if i < 3 else nc.gpsimd
-            queue.dma_start(out=ds_win[:].bitcast(I32)[i:P:32, :], in_=ds_rows[i:16:4, :])
 
         xs_g = keep.tile([P, S], U8, name="xs_g")
         nc.vector.tensor_copy(out=xs_g[:], in_=xs_win[:].indirect(offs_t[:]))
         xs_p = keep.tile([P, S], U8, name="xs_p", align_bytes=64)
-        nc.vector.tensor_copy(out=xs_p[:].bitcast(I32), in_=xs_g[:].bitcast(I32))
-        for c in range(2):
-            nc.scalar.dma_start(
-                out=xs_p[:].bitcast(I32)[2 + c : P : 32, :], in_=xs_g[:].bitcast(I32)[16 + c : P : 32, :]
-            )
+        place_scale_rows(nc, xs_p, xs_g)
+        ds_g = keep.tile([P, H], U8, name="ds_g")
+        nc.vector.tensor_copy(
+            out=ds_g[:].rearrange("p (t m) -> p m t", t=PACK), in_=ds_win[:].indirect(ci_t[:])
+        )
+        ds_p = keep.tile([P, H], U8, name="ds_p", align_bytes=64)
+        place_scale_rows(nc, ds_p, ds_g)
         dw_g = keep.tile([P, H], U32, name="dw_g", tag="slot_a", align_bytes=64)
         nc.vector.tensor_copy(
             out=dw_g[:].rearrange("p (t m) -> p m t", t=PACK), in_=dw_win[:].bitcast(U32).indirect(ci_t[:])
-        )
-        ds_g = keep.tile([P, H], U8, name="ds_g", align_bytes=64)
-        nc.vector.tensor_copy(
-            out=ds_g[:].rearrange("p (t m) -> p m t", t=PACK), in_=ds_win[:].indirect(ci_t[:])
         )
         xw_g = keep.tile([P, S], U32, name="xw_g", tag="slot_b", align_bytes=64)
         nc.vector.tensor_copy(out=xw_g[:], in_=xw_win[:].bitcast(U32).indirect(offs_t[:]))
@@ -97,7 +99,7 @@ def tile_picked_hwlsendhoperl_none_p_kernel(
             nc.tensor.matmul_mx(
                 out=s_ps[:],
                 lhsT=dw_g[:, cols].bitcast(FP8X4),
-                lhsT_scale=ds_g[:, cols],
+                lhsT_scale=ds_p[:, cols],
                 rhs=xw_g[:].bitcast(FP8X4),
                 rhs_scale=xs_p[:],
                 start=True,

@@ -49,6 +49,10 @@ def tile_picked_hwlsendhoperl_none_p_kernel(
         ds_win = keep.tile([P, T], U8, name="ds_win", tag="slot_b", align_bytes=64)
         xw_win = keep.tile([P, T], I32, name="xw_win", tag="slot_d")
         dw_win = keep.tile([P, T], I32, name="dw_win", tag="slot_c")
+        warm_in = keep.tile([P, 1], F32, name="warm_in")
+        warm_out = keep.tile([P, 1], F32, name="warm_out")
+        nc.gpsimd.memset(warm_in[:], 0.0)
+        nc.scalar.activation(out=warm_out[:], in_=warm_in[:], func=ACT.Sigmoid)
         nc.vector.memset(xs_win[:].bitcast(I32), 0)
         nc.vector.memset(ds_win[:].bitcast(I32), 0)
         nc.sync.dma_start(out=offs_t[:], in_=offs)

@@ -13,15 +13,28 @@ ALU = mybir.AluOpType
 ACT = mybir.ActivationFunctionType
 
 P = 128
+K = 512
 T = 2048
 S = 256
 H = 512
 N = 512
 PACK = 4
+OUT_TILES = N // P
+STRIPE = 16
 WIN = 2 * S
-HALF = S // 2
 EARLY = T // 4
-FLOPS = 2 * 512 * H * S + 2 * H * N * S
+ALL = slice(0, S)
+HALVES = [slice(0, S // 2), slice(S // 2, S)]
+PIECES = [slice(0, S // 4), slice(S // 4, S // 2), slice(S // 2, S)]
+FLOPS = 2 * K * H * S + 2 * H * N * S
+
+
+def width(cols):
+    return cols.stop - cols.start
+
+
+def entries(list_tile, cols):
+    return list_tile[:, cols.start // STRIPE : cols.stop // STRIPE]
 
 
 def place_scale_rows(nc, placed, gathered):
@@ -38,21 +51,23 @@ def tile_picked_hwlsendhoperl_none_p_kernel(
         keep = ctx.enter_context(tc.tile_pool(name="keep", bufs=1))
         psum = ctx.enter_context(tc.psum_pool(name="psum", bufs=1))
 
-        offs_t = keep.tile([P, S // 16], U16, name="offs_t")
-        ci_t = keep.tile([P, H // 16], U16, name="ci_t")
-        n1_t = keep.tile([P, S // 16], U16, name="n1_t")
-        n2_t = keep.tile([P, S // 16], U16, name="n2_t")
-        n3_t = keep.tile([P, S // 16], U16, name="n3_t")
-        n4_t = keep.tile([P, S // 16], U16, name="n4_t")
+        offs_t = keep.tile([P, S // STRIPE], U16, name="offs_t")
+        ci_t = keep.tile([P, H // STRIPE], U16, name="ci_t")
+        n1_t = keep.tile([P, S // STRIPE], U16, name="n1_t")
+        n2_t = keep.tile([P, S // STRIPE], U16, name="n2_t")
+        n3_t = keep.tile([P, S // STRIPE], U16, name="n3_t")
+        n4_t = keep.tile([P, S // STRIPE], U16, name="n4_t")
 
         xs_win = keep.tile([P, T], U8, name="xs_win", tag="slot_a", align_bytes=64)
         ds_win = keep.tile([P, T], U8, name="ds_win", tag="slot_b", align_bytes=64)
         xw_win = keep.tile([P, T], I32, name="xw_win", tag="slot_d")
         dw_win = keep.tile([P, T], I32, name="dw_win", tag="slot_c")
+
         warm_in = keep.tile([P, 1], F32, name="warm_in")
         warm_out = keep.tile([P, 1], F32, name="warm_out")
         nc.gpsimd.memset(warm_in[:], 0.0)
         nc.scalar.activation(out=warm_out[:], in_=warm_in[:], func=ACT.Sigmoid)
+
         nc.vector.memset(xs_win[:].bitcast(I32), 0)
         nc.vector.memset(ds_win[:].bitcast(I32), 0)
         nc.sync.dma_start(out=offs_t[:], in_=offs)
@@ -89,114 +104,143 @@ def tile_picked_hwlsendhoperl_none_p_kernel(
         nc.sync.dma_start(out=w_raw[:], in_=w1.rearrange("(p j) n -> p j n", j=PACK))
         rowvals = keep.tile([P, 3, 8, 1], F32, name="rowvals", tag="slot_d")
         gn_t = rowvals[:, 0, :PACK, :]
-        sl_t = rowvals[:, 1, :PACK, :]
-        th_t = rowvals[:, 2, :PACK, :]
+        sl_t = rowvals[:, 1, :OUT_TILES, :]
+        th_t = rowvals[:, 2, :OUT_TILES, :]
         with nc.allow_non_contiguous_dma(reason="one value a row"):
             nc.sync.dma_start(out=gn_t, in_=gn.rearrange("(p j) o -> p j o", j=PACK))
             nc.sync.dma_start(out=sl_t, in_=sl.rearrange("(u p) o -> p u o", p=P))
             nc.sync.dma_start(out=th_t, in_=th.rearrange("(u p) o -> p u o", p=P))
 
-        s_win = []
-        for t in range(PACK):
-            cols = slice(t * P, (t + 1) * P)
-            s_ps = psum.tile([P, S], F32, name=f"s_ps{t}", tag=f"bank{t}")
+        s_win = [keep.tile([P, WIN], F32, name=f"s_win{t}") for t in range(PACK)]
+
+        def first_product(t, cols, bank):
+            rows = slice(t * P, (t + 1) * P)
+            s_ps = psum.tile([P, width(cols)], F32, name=f"s_ps{bank}", tag=f"bank{bank}")
             nc.tensor.matmul_mx(
                 out=s_ps[:],
-                lhsT=dw_g[:, cols].bitcast(FP8X4),
-                lhsT_scale=ds_p[:, cols],
-                rhs=xw_g[:].bitcast(FP8X4),
-                rhs_scale=xs_p[:],
+                lhsT=dw_g[:, rows].bitcast(FP8X4),
+                lhsT_scale=ds_p[:, rows],
+                rhs=xw_g[:, cols].bitcast(FP8X4),
+                rhs_scale=xs_p[:, cols],
                 start=True,
                 stop=True,
             )
-            win = keep.tile([P, WIN], F32, name=f"s_win{t}")
-            nc.vector.tensor_scalar(
-                out=win[:, :S], in0=s_ps[:], scalar1=0.0625, scalar2=None, op0=ALU.mult
-            )
-            s_win.append(win)
+            if cols.start == 0:
+                nc.vector.tensor_scalar(
+                    out=s_win[t][:, cols], in0=s_ps[:], scalar1=0.0625, scalar2=None, op0=ALU.mult
+                )
+            else:
+                nc.scalar.activation(out=s_win[t][:, cols], in_=s_ps[:], func=ACT.Copy, scale=0.0625)
+
+        spare_bank = PACK + len(PIECES)
+        first_product(0, HALVES[0], 0)
+        first_product(0, HALVES[1], spare_bank)
+        for t in range(1, PACK):
+            first_product(t, ALL, t)
+
         fetched = keep.tile([P, PACK, S], F32, name="fetched", tag="stage", align_bytes=64)
         for t in range(PACK):
             nc.scalar.activation(out=fetched[:, t, :], in_=s_win[t][:].indirect(n1_t[:]), func=ACT.Copy)
         st = []
         for t in range(PACK):
-            m = keep.tile([P, S], F32, name=f"st{t}")
-            nc.vector.tensor_tensor(out=m[:], in0=s_win[t][:, :S], in1=fetched[:, t, :], op=ALU.max)
-            st.append(m)
+            larger = keep.tile([P, S], F32, name=f"st{t}")
+            nc.vector.tensor_tensor(out=larger[:], in0=s_win[t][:, ALL], in1=fetched[:, t, :], op=ALU.max)
+            st.append(larger)
         sent = []
         for t in range(PACK):
-            win = keep.tile([P, WIN], F32, name=f"sent{t}")
-            nc.scalar.activation(out=win[:].indirect(n2_t[:]), in_=st[t][:], func=ACT.Copy)
-            sent.append(win)
+            sent_win = keep.tile([P, WIN], F32, name=f"sent{t}")
+            nc.scalar.activation(out=sent_win[:].indirect(n2_t[:]), in_=st[t][:], func=ACT.Copy)
+            sent.append(sent_win)
 
         w_codes = keep.tile([P, N], U32, name="w_codes", align_bytes=64)
         w_scales = keep.tile([P, N], U8, name="w_scales", align_bytes=64)
         w_bf = keep.tile([P, N, PACK], BF16, name="w_bf", tag="stage", align_bytes=64)
-        for u in range(PACK):
-            cols = slice(u * P, (u + 1) * P)
+        for u in range(OUT_TILES):
+            w_cols = slice(u * P, (u + 1) * P)
             nc.vector.tensor_copy(
-                out=w_bf[:, cols, :].rearrange("p (c i) j -> p c j i", i=4),
-                in_=w_raw[:, :, cols].rearrange("p j (c i) -> p c j i", i=4),
+                out=w_bf[:, w_cols, :].rearrange("p (c i) j -> p c j i", i=4),
+                in_=w_raw[:, :, w_cols].rearrange("p j (c i) -> p c j i", i=4),
             )
         nc.vector.quantize_mx(
             out=w_codes[:].bitcast(FP8X4), scales=w_scales[:], in_=w_bf[:].rearrange("p c j -> p (c j)")
         )
-        bias_t = keep.tile([P, PACK, 1], F32, name="bias_t")
-        slth = keep.tile([P, PACK, 1], F32, name="slth")
+
+        bias_t = keep.tile([P, OUT_TILES, 1], F32, name="bias_t")
+        slth = keep.tile([P, OUT_TILES, 1], F32, name="slth")
         nc.gpsimd.tensor_tensor(out=slth[:], in0=sl_t, in1=th_t, op=ALU.mult)
         nc.gpsimd.tensor_scalar(out=bias_t[:], in0=slth[:], scalar1=-1.0, scalar2=0.0, op0=ALU.mult, op1=ALU.add)
 
-        halves = [slice(0, HALF), slice(HALF, S)]
-        z_bf = [keep.tile([P, HALF, PACK], BF16, name=f"z_bf{a}", align_bytes=64) for a in range(2)]
-        diff = keep.tile([P, PACK, S], F32, name="diff", tag="stage", align_bytes=64)
+        z_bf = [
+            keep.tile([P, width(cols), PACK], BF16, name=f"z_bf{a}", align_bytes=64)
+            for a, cols in enumerate(PIECES)
+        ]
+        gained = keep.tile([P, PACK, S], F32, name="gained", tag="stage", align_bytes=64)
         for t in range(PACK):
-            for a in range(2):
-                nc.vector.tensor_tensor(
-                    out=diff[:, t, halves[a]], in0=sent[t][:, halves[a]], in1=s_win[t][:, halves[a]], op=ALU.subtract
-                )
-            for a in range(2):
-                nc.vector.tensor_scalar(
-                    out=z_bf[a][:, :, t], in0=diff[:, t, halves[a]], scalar1=gn_t[:, t, :], scalar2=None, op0=ALU.mult
-                )
-        h_sb = [keep.tile([P, S], F32, name=f"h_sb{u}") for u in range(PACK)]
-        for a in range(2):
-            z_codes = keep.tile([P, HALF], U32, name=f"z_codes{a}", align_bytes=64)
-            z_scales = keep.tile([P, HALF], U8, name=f"z_scales{a}", align_bytes=64)
+            nc.vector.tensor_scalar(
+                out=gained[:, t, :], in0=s_win[t][:, ALL], scalar1=gn_t[:, t, :], scalar2=None, op0=ALU.mult
+            )
+
+        def make_z(t, a):
+            nc.vector.scalar_tensor_tensor(
+                out=z_bf[a][:, :, t],
+                in0=sent[t][:, PIECES[a]],
+                scalar=gn_t[:, t, :],
+                in1=gained[:, t, PIECES[a]],
+                op0=ALU.mult,
+                op1=ALU.subtract,
+            )
+
+        for t in range(PACK - 1):
+            for a in range(len(PIECES)):
+                make_z(t, a)
+
+        z_codes = keep.tile([P, S], U32, name="z_codes", align_bytes=64)
+        z_scales = keep.tile([P, S], U8, name="z_scales", align_bytes=64)
+        h_sb = [keep.tile([P, S], F32, name=f"h_sb{u}") for u in range(OUT_TILES)]
+
+        def second_product(u, cols, bank):
+            rows = slice(u * P, (u + 1) * P)
+            h_ps = psum.tile([P, width(cols)], F32, name=f"h_ps{bank}", tag=f"bank{bank}")
+            nc.tensor.matmul_mx(
+                out=h_ps[:],
+                lhsT=w_codes[:, rows].bitcast(FP8X4),
+                lhsT_scale=w_scales[:, rows],
+                rhs=z_codes[:, cols].bitcast(FP8X4),
+                rhs_scale=z_scales[:, cols],
+                start=True,
+                stop=True,
+            )
+            if u == 0 and cols.start == 0:
+                nc.scalar.copy(out=h_sb[u][:, cols], in_=h_ps[:])
+            else:
+                nc.vector.tensor_copy(out=h_sb[u][:, cols], in_=h_ps[:])
+
+        for a, cols in enumerate(PIECES):
+            make_z(PACK - 1, a)
             nc.vector.quantize_mx(
-                out=z_codes[:].bitcast(FP8X4),
-                scales=z_scales[:],
+                out=z_codes[:, cols].bitcast(FP8X4),
+                scales=z_scales[:, cols],
                 in_=z_bf[a][:].rearrange("p c j -> p (c j)"),
             )
-            for u in range(PACK):
-                cols = slice(u * P, (u + 1) * P)
-                h_ps = psum.tile([P, HALF], F32, name=f"h_ps{a}{u}", tag=f"bank{(1 - a) * PACK + u}")
-                nc.tensor.matmul_mx(
-                    out=h_ps[:],
-                    lhsT=w_codes[:, cols].bitcast(FP8X4),
-                    lhsT_scale=w_scales[:, cols],
-                    rhs=z_codes[:].bitcast(FP8X4),
-                    rhs_scale=z_scales[:],
-                    start=True,
-                    stop=True,
-                )
-                nc.vector.tensor_copy(out=h_sb[u][:, halves[a]], in_=h_ps[:])
+            second_product(0, cols, PACK + a)
+        for u in range(1, OUT_TILES):
+            second_product(u, ALL, u)
 
-        for u in range(PACK):
-            win = keep.tile([P, WIN], F32, name=f"sent2_{u}")
-            if u == 0:
-                for a in range(2):
-                    nc.scalar.activation(
-                        out=win[:].indirect(n3_t[:, a * 8 : (a + 1) * 8]), in_=h_sb[u][:, halves[a]], func=ACT.Copy
-                    )
-            else:
-                nc.scalar.activation(out=win[:].indirect(n3_t[:]), in_=h_sb[u][:], func=ACT.Copy)
+        for u in range(OUT_TILES):
+            sent2_win = keep.tile([P, WIN], F32, name=f"sent2_{u}")
+            for cols in PIECES if u == 0 else [ALL]:
+                nc.scalar.activation(
+                    out=sent2_win[:].indirect(entries(n3_t, cols)), in_=h_sb[u][:, cols], func=ACT.Copy
+                )
             sg = keep.tile([P, S], F32, name=f"sg{u}")
-            nc.scalar.activation(
-                out=sg[:],
-                in_=win[:].indirect(n4_t[:]),
-                func=ACT.Sigmoid,
-                scale=sl_t[:, u, :],
-                bias=bias_t[:, u, :],
-            )
             res = keep.tile([P, S], F32, name=f"res{u}")
-            nc.vector.tensor_tensor(out=res[:], in0=h_sb[u][:], in1=sg[:], op=ALU.mult)
-            nc.sync.dma_start(out=out[u * P : (u + 1) * P, :], in_=res[:])
+            for cols in HALVES if u == OUT_TILES - 1 else [ALL]:
+                nc.scalar.activation(
+                    out=sg[:, cols],
+                    in_=sent2_win[:].indirect(entries(n4_t, cols)),
+                    func=ACT.Sigmoid,
+                    scale=sl_t[:, u, :],
+                    bias=bias_t[:, u, :],
+                )
+                nc.vector.tensor_tensor(out=res[:, cols], in0=h_sb[u][:, cols], in1=sg[:, cols], op=ALU.mult)
+                nc.sync.dma_start(out=out[u * P : (u + 1) * P, cols], in_=res[:, cols])

from contextlib import ExitStack

import concourse.mybir as mybir

F32 = mybir.dt.float32
BF16 = mybir.dt.bfloat16
I32 = mybir.dt.int32
U32 = mybir.dt.uint32
U16 = mybir.dt.uint16
U8 = mybir.dt.uint8
FP8X4 = mybir.dt.float8_e4m3fn_x4
ALU = mybir.AluOpType
ACT = mybir.ActivationFunctionType

P = 128
K = 512
T = 2048
S = 256
H = 512
N = 512
PACK = 4
OUT_TILES = N // P
STRIPE = 16
WIN = 2 * S
EARLY = T // 4
ALL = slice(0, S)
HALVES = [slice(0, S // 2), slice(S // 2, S)]
PIECES = [slice(0, S // 4), slice(S // 4, S // 2), slice(S // 2, S)]
FLOPS = 2 * K * H * S + 2 * H * N * S


def width(cols):
    return cols.stop - cols.start


def entries(list_tile, cols):
    return list_tile[:, cols.start // STRIPE : cols.stop // STRIPE]


def place_scale_rows(nc, placed, gathered):
    nc.vector.tensor_copy(out=placed[:].bitcast(I32), in_=gathered[:].bitcast(I32))
    for i in range(1, 4):
        nc.sync.dma_start(out=placed[:].bitcast(I32)[i:P:32, :], in_=gathered[:].bitcast(I32)[8 * i : P : 32, :])


def tile_picked_hwlsendhoperl_none_p_kernel(
    tc, x_words, x_scales, d_words, d_scales, gn, w1, sl, th, offs, ci, n1, n2, n3, n4, out
):
    nc = tc.nc
    with ExitStack() as ctx:
        keep = ctx.enter_context(tc.tile_pool(name="keep", bufs=1))
        psum = ctx.enter_context(tc.psum_pool(name="psum", bufs=1))

        offs_t = keep.tile([P, S // STRIPE], U16, name="offs_t")
        ci_t = keep.tile([P, H // STRIPE], U16, name="ci_t")
        n1_t = keep.tile([P, S // STRIPE], U16, name="n1_t")
        n2_t = keep.tile([P, S // STRIPE], U16, name="n2_t")
        n3_t = keep.tile([P, S // STRIPE], U16, name="n3_t")
        n4_t = keep.tile([P, S // STRIPE], U16, name="n4_t")

        xs_win = keep.tile([P, T], U8, name="xs_win", tag="slot_a", align_bytes=64)
        ds_win = keep.tile([P, T], U8, name="ds_win", tag="slot_b", align_bytes=64)
        xw_win = keep.tile([P, T], I32, name="xw_win", tag="slot_d")
        dw_win = keep.tile([P, T], I32, name="dw_win", tag="slot_c")

        warm_in = keep.tile([P, 1], F32, name="warm_in")
        warm_out = keep.tile([P, 1], F32, name="warm_out")
        nc.gpsimd.memset(warm_in[:], 0.0)
        nc.scalar.activation(out=warm_out[:], in_=warm_in[:], func=ACT.Sigmoid)

        nc.vector.memset(xs_win[:].bitcast(I32), 0)
        nc.vector.memset(ds_win[:].bitcast(I32), 0)
        nc.sync.dma_start(out=offs_t[:], in_=offs)
        nc.sync.dma_start(out=ci_t[:], in_=ci)
        d_rows = d_words[0].rearrange("p c r -> p (c r)").bitcast(I32)
        nc.sync.dma_start(out=dw_win[:, :EARLY], in_=d_rows[:, :EARLY])
        nc.sync.dma_start(out=xs_win[:].bitcast(I32)[0:P:8, :], in_=x_scales[0].bitcast(I32))
        nc.sync.dma_start(out=ds_win[:].bitcast(I32)[0:P:8, :], in_=d_scales[0].bitcast(I32))
        nc.sync.dma_start(out=dw_win[:, EARLY:], in_=d_rows[:, EARLY:])
        nc.sync.dma_start(out=n1_t[:], in_=n1)
        nc.sync.dma_start(out=n2_t[:], in_=n2)
        nc.sync.dma_start(out=n3_t[:], in_=n3)
        nc.sync.dma_start(out=xw_win[:], in_=x_words[0].rearrange("p c r -> p (c r)").bitcast(I32))
        nc.sync.dma_start(out=n4_t[:], in_=n4)

        xs_g = keep.tile([P, S], U8, name="xs_g")
        nc.vector.tensor_copy(out=xs_g[:], in_=xs_win[:].indirect(offs_t[:]))
        xs_p = keep.tile([P, S], U8, name="xs_p", align_bytes=64)
        place_scale_rows(nc, xs_p, xs_g)
        ds_g = keep.tile([P, H], U8, name="ds_g")
        nc.vector.tensor_copy(
            out=ds_g[:].rearrange("p (t m) -> p m t", t=PACK), in_=ds_win[:].indirect(ci_t[:])
        )
        ds_p = keep.tile([P, H], U8, name="ds_p", align_bytes=64)
        place_scale_rows(nc, ds_p, ds_g)
        dw_g = keep.tile([P, H], U32, name="dw_g", tag="slot_a", align_bytes=64)
        nc.vector.tensor_copy(
            out=dw_g[:].rearrange("p (t m) -> p m t", t=PACK), in_=dw_win[:].bitcast(U32).indirect(ci_t[:])
        )
        xw_g = keep.tile([P, S], U32, name="xw_g", tag="slot_b", align_bytes=64)
        nc.vector.tensor_copy(out=xw_g[:], in_=xw_win[:].bitcast(U32).indirect(offs_t[:]))

        w_raw = keep.tile([P, PACK, N], F32, name="w_raw", tag="slot_c")
        nc.sync.dma_start(out=w_raw[:], in_=w1.rearrange("(p j) n -> p j n", j=PACK))
        rowvals = keep.tile([P, 3, 8, 1], F32, name="rowvals", tag="slot_d")
        gn_t = rowvals[:, 0, :PACK, :]
        sl_t = rowvals[:, 1, :OUT_TILES, :]
        th_t = rowvals[:, 2, :OUT_TILES, :]
        with nc.allow_non_contiguous_dma(reason="one value a row"):
            nc.sync.dma_start(out=gn_t, in_=gn.rearrange("(p j) o -> p j o", j=PACK))
            nc.sync.dma_start(out=sl_t, in_=sl.rearrange("(u p) o -> p u o", p=P))
            nc.sync.dma_start(out=th_t, in_=th.rearrange("(u p) o -> p u o", p=P))

        s_win = [keep.tile([P, WIN], F32, name=f"s_win{t}") for t in range(PACK)]

        def first_product(t, cols, bank):
            rows = slice(t * P, (t + 1) * P)
            s_ps = psum.tile([P, width(cols)], F32, name=f"s_ps{bank}", tag=f"bank{bank}")
            nc.tensor.matmul_mx(
                out=s_ps[:],
                lhsT=dw_g[:, rows].bitcast(FP8X4),
                lhsT_scale=ds_p[:, rows],
                rhs=xw_g[:, cols].bitcast(FP8X4),
                rhs_scale=xs_p[:, cols],
                start=True,
                stop=True,
            )
            if cols.start == 0:
                nc.vector.tensor_scalar(
                    out=s_win[t][:, cols], in0=s_ps[:], scalar1=0.0625, scalar2=None, op0=ALU.mult
                )
            else:
                nc.scalar.activation(out=s_win[t][:, cols], in_=s_ps[:], func=ACT.Copy, scale=0.0625)

        spare_bank = PACK + len(PIECES)
        first_product(0, HALVES[0], 0)
        first_product(0, HALVES[1], spare_bank)
        for t in range(1, PACK):
            first_product(t, ALL, t)

        fetched = keep.tile([P, PACK, S], F32, name="fetched", tag="stage", align_bytes=64)
        for t in range(PACK):
            nc.scalar.activation(out=fetched[:, t, :], in_=s_win[t][:].indirect(n1_t[:]), func=ACT.Copy)
        st = []
        for t in range(PACK):
            larger = keep.tile([P, S], F32, name=f"st{t}")
            nc.vector.tensor_tensor(out=larger[:], in0=s_win[t][:, ALL], in1=fetched[:, t, :], op=ALU.max)
            st.append(larger)
        sent = []
        for t in range(PACK):
            sent_win = keep.tile([P, WIN], F32, name=f"sent{t}")
            nc.scalar.activation(out=sent_win[:].indirect(n2_t[:]), in_=st[t][:], func=ACT.Copy)
            sent.append(sent_win)

        w_codes = keep.tile([P, N], U32, name="w_codes", align_bytes=64)
        w_scales = keep.tile([P, N], U8, name="w_scales", align_bytes=64)
        w_bf = keep.tile([P, N, PACK], BF16, name="w_bf", tag="stage", align_bytes=64)
        for u in range(OUT_TILES):
            w_cols = slice(u * P, (u + 1) * P)
            nc.vector.tensor_copy(
                out=w_bf[:, w_cols, :].rearrange("p (c i) j -> p c j i", i=4),
                in_=w_raw[:, :, w_cols].rearrange("p j (c i) -> p c j i", i=4),
            )
        nc.vector.quantize_mx(
            out=w_codes[:].bitcast(FP8X4), scales=w_scales[:], in_=w_bf[:].rearrange("p c j -> p (c j)")
        )

        bias_t = keep.tile([P, OUT_TILES, 1], F32, name="bias_t")
        slth = keep.tile([P, OUT_TILES, 1], F32, name="slth")
        nc.gpsimd.tensor_tensor(out=slth[:], in0=sl_t, in1=th_t, op=ALU.mult)
        nc.gpsimd.tensor_scalar(out=bias_t[:], in0=slth[:], scalar1=-1.0, scalar2=0.0, op0=ALU.mult, op1=ALU.add)

        z_bf = [
            keep.tile([P, width(cols), PACK], BF16, name=f"z_bf{a}", align_bytes=64)
            for a, cols in enumerate(PIECES)
        ]
        gained = keep.tile([P, PACK, S], F32, name="gained", tag="stage", align_bytes=64)
        for t in range(PACK):
            nc.vector.tensor_scalar(
                out=gained[:, t, :], in0=s_win[t][:, ALL], scalar1=gn_t[:, t, :], scalar2=None, op0=ALU.mult
            )

        def make_z(t, a):
            nc.vector.scalar_tensor_tensor(
                out=z_bf[a][:, :, t],
                in0=sent[t][:, PIECES[a]],
                scalar=gn_t[:, t, :],
                in1=gained[:, t, PIECES[a]],
                op0=ALU.mult,
                op1=ALU.subtract,
            )

        for t in range(PACK - 1):
            for a in range(len(PIECES)):
                make_z(t, a)

        z_codes = keep.tile([P, S], U32, name="z_codes", align_bytes=64)
        z_scales = keep.tile([P, S], U8, name="z_scales", align_bytes=64)
        h_sb = [keep.tile([P, S], F32, name=f"h_sb{u}") for u in range(OUT_TILES)]

        def second_product(u, cols, bank):
            rows = slice(u * P, (u + 1) * P)
            h_ps = psum.tile([P, width(cols)], F32, name=f"h_ps{bank}", tag=f"bank{bank}")
            nc.tensor.matmul_mx(
                out=h_ps[:],
                lhsT=w_codes[:, rows].bitcast(FP8X4),
                lhsT_scale=w_scales[:, rows],
                rhs=z_codes[:, cols].bitcast(FP8X4),
                rhs_scale=z_scales[:, cols],
                start=True,
                stop=True,
            )
            if u == 0 and cols.start == 0:
                nc.scalar.copy(out=h_sb[u][:, cols], in_=h_ps[:])
            else:
                nc.vector.tensor_copy(out=h_sb[u][:, cols], in_=h_ps[:])

        for a, cols in enumerate(PIECES):
            make_z(PACK - 1, a)
            nc.vector.quantize_mx(
                out=z_codes[:, cols].bitcast(FP8X4),
                scales=z_scales[:, cols],
                in_=z_bf[a][:].rearrange("p c j -> p (c j)"),
            )
            second_product(0, cols, PACK + a)
        for u in range(1, OUT_TILES):
            second_product(u, ALL, u)

        for u in range(OUT_TILES):
            sent2_win = keep.tile([P, WIN], F32, name=f"sent2_{u}")
            for cols in PIECES if u == 0 else [ALL]:
                nc.scalar.activation(
                    out=sent2_win[:].indirect(entries(n3_t, cols)), in_=h_sb[u][:, cols], func=ACT.Copy
                )
            sg = keep.tile([P, S], F32, name=f"sg{u}")
            res = keep.tile([P, S], F32, name=f"res{u}")
            for cols in HALVES if u == OUT_TILES - 1 else [ALL]:
                nc.scalar.activation(
                    out=sg[:, cols],
                    in_=sent2_win[:].indirect(entries(n4_t, cols)),
                    func=ACT.Sigmoid,
                    scale=sl_t[:, u, :],
                    bias=bias_t[:, u, :],
                )
                nc.vector.tensor_tensor(out=res[:, cols], in0=h_sb[u][:, cols], in1=sg[:, cols], op=ALU.mult)
                nc.sync.dma_start(out=out[u * P : (u + 1) * P, cols], in_=res[:, cols])
